import numpy as np
import ml_dtypes


def mxq(x, axis, fmt="e4m3"):
    dtype, down = {"e4m3": (ml_dtypes.float8_e4m3fn, 7), "e5m2": (ml_dtypes.float8_e5m2, 14)}[fmt]
    v = np.moveaxis(np.asarray(x, np.float32).astype(ml_dtypes.bfloat16).astype(np.float64), axis, -1)
    blocks = v.reshape(v.shape[:-1] + (-1, 32))
    amax = np.abs(blocks).max(-1, keepdims=True)
    byte = np.maximum(np.where(amax > 0, np.frexp(amax)[1] - 1 + 127, 0) - down, 1)
    scale = np.exp2(byte - 127.0)
    codes = (blocks / scale).astype(np.float32).astype(dtype).astype(np.float64)
    return np.moveaxis((codes * scale).reshape(v.shape), -1, axis)


WIDE = False


def mx_kscale(k, group=512):
    if not WIDE:
        return np.ones(k)
    levels = np.array([18, -18])
    if group != 512:
        return np.exp2(np.random.permutation(np.resize(levels, k // group))).repeat(group)
    if k % 512:
        return np.exp2(np.random.permutation(np.resize(levels, k // 32))).repeat(32)
    a = np.empty((k // 512, 16))
    for p in range(k // 512):
        a[p, :8] = np.random.permutation(np.resize(levels, 8))
        for g in range(8):
            far = levels[np.abs(levels - a[p, g]) >= 10]
            a[p, g + 8] = far[np.random.randint(len(far))]
    return np.exp2(a.ravel()).repeat(32)


def f64(x):
    return np.asarray(x).astype(np.float64)


G, D, M, N = 4, 128, 128, 1024


def setup_inputs():
    n = np.random.standard_normal
    s = mx_kscale(D, 0)[:, None]
    return {
        "x": (n((G, D, N)) * s).astype(np.float32),
        "w": (n((G, D, M)) / np.sqrt(D) / s).astype(np.float32),
        "r": n((G, M, N)).astype(np.float32),
    }


def reference(x, w, r):
    xq = mxq(f64(x), 1, "e4m3")
    y = mxq(f64(w), 1, "e4m3").transpose(0, 2, 1) @ xq
    y = 1.0 / (1.0 + np.exp(-(y)))
    y = y + f64(r)
    return y

@@ -1,0 +1,135 @@
+from contextlib import ExitStack
+
+import concourse.mybir as mybir
+
+G, D, M, N = 4, 128, 128, 1024
+FLOPS = 2 * G * D * M * N
+
+F32 = mybir.dt.float32
+BF16 = mybir.dt.bfloat16
+U32 = mybir.dt.uint32
+U8 = mybir.dt.uint8
+FP8X4 = mybir.dt.float8_e4m3fn_x4
+SIGMOID = mybir.ActivationFunctionType.Sigmoid
+COPY = mybir.ActivationFunctionType.Copy
+ADD = mybir.AluOpType.add
+
+P = 128
+PACK = 4
+ROWS = D // PACK
+HALF = 512
+HALVES = N // HALF
+QUART = 256
+SPLIT = 352
+
+
+def interleave(nc, dst, src):
+    nc.vector.tensor_copy(
+        out=dst.rearrange("p (c i) j -> p c j i", i=4),
+        in_=src.rearrange("p j (c i) -> p c j i", i=4),
+    )
+
+
+def interleave_s(nc, dst, src):
+    nc.scalar.copy(
+        out=dst.rearrange("p (c i) j -> p c j i", i=4),
+        in_=src.rearrange("p j (c i) -> p c j i", i=4),
+    )
+
+
+def quantize(nc, codes, scales, src):
+    nc.vector.quantize_mx(out=codes.bitcast(FP8X4), scales=scales, in_=src.rearrange("p n j -> p (n j)"))
+
+
+def tile_rows_glin_sigmoid_res_kernel(tc, x, w, r, out):
+    nc = tc.nc
+    x_rows = x.rearrange("g (p j) n -> (g p) j n", j=PACK)
+    w_rows = w.rearrange("g (p j) m -> (g p) j m", j=PACK)
+
+    with ExitStack() as ctx:
+        sb = ctx.enter_context(tc.tile_pool(name="sb", bufs=1))
+        ps = ctx.enter_context(tc.psum_pool(name="ps", bufs=1))
+        ctx.enter_context(tc.manual_schedule())
+
+        x_raw = [sb.tile([P, PACK, HALF], F32, name="x_raw%d" % h) for h in range(HALVES)]
+        w_raw = sb.tile([P, PACK, M], F32)
+        r_sb = [sb.tile([P, N], F32, name="r_sb%d" % g) for g in range(G)]
+        x_bf = [sb.tile([P, HALF, PACK], BF16, name="x_bf%d" % h, align_bytes=64) for h in range(HALVES)]
+        w_bf = sb.tile([P, M, PACK], BF16, align_bytes=64)
+        x_codes = [sb.tile([P, HALF], U32, name="x_codes%d" % h, align_bytes=64) for h in range(HALVES)]
+        x_scales = [sb.tile([P, HALF], U8, name="x_scales%d" % h, align_bytes=64) for h in range(HALVES)]
+        w_codes = sb.tile([P, M], U32, align_bytes=64)
+        w_scales = sb.tile([P, M], U8, align_bytes=64)
+        sig = [sb.tile([P, N], F32, name="sig%d" % g) for g in range(G)]
+        res = [sb.tile([P, N], F32, name="res%d" % g) for g in range(G)]
+        z = [[ps.tile([P, HALF], F32, name="z%d_%d" % (g, h)) for h in range(HALVES)] for g in range(G)]
+
+        def cols(h):
+            return slice(h * HALF, (h + 1) * HALF)
+
+        def matmul(g, h):
+            rows = slice(g * ROWS, (g + 1) * ROWS)
+            nc.tensor.matmul_mx(
+                out=z[g][h][:],
+                lhsT=w_codes[rows, :].bitcast(FP8X4),
+                lhsT_scale=w_scales[rows, :],
+                rhs=x_codes[h][rows, :].bitcast(FP8X4),
+                rhs_scale=x_scales[h][rows, :],
+                start=True,
+                stop=True,
+            )
+
+        def sigmoid(g, h):
+            nc.scalar.activation(out=sig[g][:, cols(h)], in_=z[g][h][:], func=SIGMOID)
+
+        def add(g, h):
+            nc.vector.tensor_tensor(out=res[g][:, cols(h)], in0=sig[g][:, cols(h)], in1=r_sb[g][:, cols(h)], op=ADD)
+
+        nc.sync.dma_start(out=x_raw[0][:], in_=x_rows[:, :, cols(0)])
+        nc.sync.dma_start(out=w_raw[:], in_=w_rows)
+        nc.sync.dma_start(out=x_raw[1][:], in_=x_rows[:, :, cols(1)])
+        for g in range(G):
+            nc.sync.dma_start(out=r_sb[g][:], in_=r[g])
+
+        def prepare(h):
+            interleave_s(nc, x_bf[h][:, SPLIT:, :], x_raw[h][:, :, SPLIT:])
+            interleave(nc, x_bf[h][:, :QUART, :], x_raw[h][:, :, :QUART])
+            interleave(nc, x_bf[h][:, QUART:SPLIT, :], x_raw[h][:, :, QUART:SPLIT])
+            quantize(nc, x_codes[h][:, :QUART], x_scales[h][:, :QUART], x_bf[h][:, :QUART, :])
+
+        def finish(h):
+            quantize(nc, x_codes[h][:, QUART:], x_scales[h][:, QUART:], x_bf[h][:, QUART:, :])
+
+        def store(g, part):
+            nc.sync.dma_start(out=out[g][:, part], in_=res[g][:, part])
+
+        prepare(0)
+        interleave(nc, w_bf[:], w_raw[:])
+        finish(0)
+        quantize(nc, w_codes[:], w_scales[:], w_bf[:])
+        for g in range(G - 1):
+            matmul(g, 0)
+        sigmoid(0, 0)
+        prepare(1)
+        finish(1)
+        sigmoid(1, 0)
+        sigmoid(2, 0)
+        for g in range(G - 1):
+            matmul(g, 1)
+            sigmoid(g, 1)
+        for h in range(HALVES):
+            matmul(G - 1, h)
+            sigmoid(G - 1, h)
+        add(0, 0)
+        store(0, cols(0))
+        add(1, 0)
+        add(0, 1)
+        store(0, cols(1))
+        add(1, 1)
+        store(1, slice(0, N))
+        add(2, 0)
+        add(2, 1)
+        store(2, slice(0, N))
+        for h in range(HALVES):
+            add(3, h)
+            store(3, cols(h))

@@ -20,18 +20,10 @@ ROWS = D // PACK
 HALF = 512
 HALVES = N // HALF
 QUART = 256
-SPLIT = 352
 
 
 def interleave(nc, dst, src):
     nc.vector.tensor_copy(
-        out=dst.rearrange("p (c i) j -> p c j i", i=4),
-        in_=src.rearrange("p j (c i) -> p c j i", i=4),
-    )
-
-
-def interleave_s(nc, dst, src):
-    nc.scalar.copy(
         out=dst.rearrange("p (c i) j -> p c j i", i=4),
         in_=src.rearrange("p j (c i) -> p c j i", i=4),
     )
@@ -92,44 +84,28 @@ def tile_rows_glin_sigmoid_res_kernel(tc, x, w, r, out):
             nc.sync.dma_start(out=r_sb[g][:], in_=r[g])
 
         def prepare(h):
-            interleave_s(nc, x_bf[h][:, SPLIT:, :], x_raw[h][:, :, SPLIT:])
-            interleave(nc, x_bf[h][:, :QUART, :], x_raw[h][:, :, :QUART])
-            interleave(nc, x_bf[h][:, QUART:SPLIT, :], x_raw[h][:, :, QUART:SPLIT])
-            quantize(nc, x_codes[h][:, :QUART], x_scales[h][:, :QUART], x_bf[h][:, :QUART, :])
+            for part in (slice(0, QUART), slice(QUART, HALF)):
+                interleave(nc, x_bf[h][:, part, :], x_raw[h][:, :, part])
 
-        def finish(h):
-            quantize(nc, x_codes[h][:, QUART:], x_scales[h][:, QUART:], x_bf[h][:, QUART:, :])
+        def finish(h, part):
+            quantize(nc, x_codes[h][:, part], x_scales[h][:, part], x_bf[h][:, part, :])
 
         def store(g, part):
             nc.sync.dma_start(out=out[g][:, part], in_=res[g][:, part])
 
         prepare(0)
         interleave(nc, w_bf[:], w_raw[:])
-        finish(0)
+        finish(0, slice(0, HALF))
         quantize(nc, w_codes[:], w_scales[:], w_bf[:])
-        for g in range(G - 1):
+        for g in range(G):
             matmul(g, 0)
-        sigmoid(0, 0)
+            sigmoid(g, 0)
         prepare(1)
-        finish(1)
-        sigmoid(1, 0)
-        sigmoid(2, 0)
-        for g in range(G - 1):
+        finish(1, slice(0, QUART))
+        finish(1, slice(QUART, HALF))
+        for g in range(G):
             matmul(g, 1)
             sigmoid(g, 1)
-        for h in range(HALVES):
-            matmul(G - 1, h)
-            sigmoid(G - 1, h)
-        add(0, 0)
-        store(0, cols(0))
-        add(1, 0)
-        add(0, 1)
-        store(0, cols(1))
-        add(1, 1)
-        store(1, slice(0, N))
-        add(2, 0)
-        add(2, 1)
-        store(2, slice(0, N))
-        for h in range(HALVES):
-            add(3, h)
-            store(3, cols(h))
+        for g, h in [(0, 0), (1, 0), (2, 0), (0, 1), (1, 1), (3, 0), (2, 1), (3, 1)]:
+            add(g, h)
+            store(g, cols(h))

@@ -20,10 +20,19 @@ ROWS = D // PACK
 HALF = 512
 HALVES = N // HALF
 QUART = 256
+SPLIT = 352
+PIECES = (((0, 0), (1, 0)), ((2, 0), (2, 1)), ((3, 0), (3, 1)), ((0, 1), (1, 1)))
 
 
 def interleave(nc, dst, src):
     nc.vector.tensor_copy(
+        out=dst.rearrange("p (c i) j -> p c j i", i=4),
+        in_=src.rearrange("p j (c i) -> p c j i", i=4),
+    )
+
+
+def interleave_s(nc, dst, src):
+    nc.scalar.copy(
         out=dst.rearrange("p (c i) j -> p c j i", i=4),
         in_=src.rearrange("p j (c i) -> p c j i", i=4),
     )
@@ -45,15 +54,15 @@ def tile_rows_glin_sigmoid_res_kernel(tc, x, w, r, out):
 
         x_raw = [sb.tile([P, PACK, HALF], F32, name="x_raw%d" % h) for h in range(HALVES)]
         w_raw = sb.tile([P, PACK, M], F32)
-        r_sb = [sb.tile([P, N], F32, name="r_sb%d" % g) for g in range(G)]
+        r_sb = [sb.tile([P, 2, HALF], F32, name="r_sb%d" % i) for i in range(len(PIECES))]
         x_bf = [sb.tile([P, HALF, PACK], BF16, name="x_bf%d" % h, align_bytes=64) for h in range(HALVES)]
         w_bf = sb.tile([P, M, PACK], BF16, align_bytes=64)
         x_codes = [sb.tile([P, HALF], U32, name="x_codes%d" % h, align_bytes=64) for h in range(HALVES)]
         x_scales = [sb.tile([P, HALF], U8, name="x_scales%d" % h, align_bytes=64) for h in range(HALVES)]
         w_codes = sb.tile([P, M], U32, align_bytes=64)
         w_scales = sb.tile([P, M], U8, align_bytes=64)
-        sig = [sb.tile([P, N], F32, name="sig%d" % g) for g in range(G)]
-        res = [sb.tile([P, N], F32, name="res%d" % g) for g in range(G)]
+        sig = [sb.tile([P, 2, HALF], F32, name="sig%d" % i) for i in range(len(PIECES))]
+        res = [sb.tile([P, 2, HALF], F32, name="res%d" % i) for i in range(len(PIECES))]
         z = [[ps.tile([P, HALF], F32, name="z%d_%d" % (g, h)) for h in range(HALVES)] for g in range(G)]
 
         def cols(h):
@@ -71,17 +80,17 @@ def tile_rows_glin_sigmoid_res_kernel(tc, x, w, r, out):
                 stop=True,
             )
 
-        def sigmoid(g, h):
-            nc.scalar.activation(out=sig[g][:, cols(h)], in_=z[g][h][:], func=SIGMOID)
-
-        def add(g, h):
-            nc.vector.tensor_tensor(out=res[g][:, cols(h)], in0=sig[g][:, cols(h)], in1=r_sb[g][:, cols(h)], op=ADD)
+        def piece_of(t, i):
+            (g0, h0), (g1, h1) = PIECES[i]
+            if g0 == g1:
+                return t[g0].rearrange("m (h n) -> m h n", h=HALVES)
+            return t[g0 : g1 + 1, :, cols(h0)].rearrange("g m n -> m g n")
 
         nc.sync.dma_start(out=x_raw[0][:], in_=x_rows[:, :, cols(0)])
         nc.sync.dma_start(out=w_raw[:], in_=w_rows)
         nc.sync.dma_start(out=x_raw[1][:], in_=x_rows[:, :, cols(1)])
-        for g in range(G):
-            nc.sync.dma_start(out=r_sb[g][:], in_=r[g])
+        for i in range(len(PIECES)):
+            nc.sync.dma_start(out=r_sb[i][:], in_=piece_of(r, i))
 
         def prepare(h):
             for part in (slice(0, QUART), slice(QUART, HALF)):
@@ -90,22 +99,24 @@ def tile_rows_glin_sigmoid_res_kernel(tc, x, w, r, out):
         def finish(h, part):
             quantize(nc, x_codes[h][:, part], x_scales[h][:, part], x_bf[h][:, part, :])
 
-        def store(g, part):
-            nc.sync.dma_start(out=out[g][:, part], in_=res[g][:, part])
-
+        warm = sb.tile([P, 8], F32)
+        nc.gpsimd.memset(warm[:], 0.0)
+        nc.scalar.activation(out=warm[:], in_=warm[:], func=SIGMOID)
         prepare(0)
         interleave(nc, w_bf[:], w_raw[:])
         finish(0, slice(0, HALF))
         quantize(nc, w_codes[:], w_scales[:], w_bf[:])
+        interleave_s(nc, x_bf[1][:, SPLIT:, :], x_raw[1][:, :, SPLIT:])
         for g in range(G):
             matmul(g, 0)
-            sigmoid(g, 0)
-        prepare(1)
+        for part in (slice(0, QUART), slice(QUART, SPLIT)):
+            interleave(nc, x_bf[1][:, part, :], x_raw[1][:, :, part])
         finish(1, slice(0, QUART))
         finish(1, slice(QUART, HALF))
-        for g in range(G):
-            matmul(g, 1)
-            sigmoid(g, 1)
-        for g, h in [(0, 0), (1, 0), (2, 0), (0, 1), (1, 1), (3, 0), (2, 1), (3, 1)]:
-            add(g, h)
-            store(g, cols(h))
+        for i, piece in enumerate(PIECES):
+            for s, (g, h) in enumerate(piece):
+                if h == 1:
+                    matmul(g, h)
+                nc.scalar.activation(out=sig[i][:, s, :], in_=z[g][h][:], func=SIGMOID)
+                nc.vector.tensor_tensor(out=res[i][:, s, :], in0=sig[i][:, s, :], in1=r_sb[i][:, s, :], op=ADD)
+            nc.sync.dma_start(out=piece_of(out, i), in_=res[i][:])

@@ -11,7 +11,6 @@ U32 = mybir.dt.uint32
 U8 = mybir.dt.uint8
 FP8X4 = mybir.dt.float8_e4m3fn_x4
 SIGMOID = mybir.ActivationFunctionType.Sigmoid
-COPY = mybir.ActivationFunctionType.Copy
 ADD = mybir.AluOpType.add
 
 P = 128
@@ -19,27 +18,12 @@ PACK = 4
 ROWS = D // PACK
 HALF = 512
 HALVES = N // HALF
-QUART = 256
-SPLIT = 352
+FIRST = 640
 PIECES = (((0, 0), (1, 0)), ((2, 0), (2, 1)), ((3, 0), (3, 1)), ((0, 1), (1, 1)))
 
 
-def interleave(nc, dst, src):
-    nc.vector.tensor_copy(
-        out=dst.rearrange("p (c i) j -> p c j i", i=4),
-        in_=src.rearrange("p j (c i) -> p c j i", i=4),
-    )
-
-
-def interleave_s(nc, dst, src):
-    nc.scalar.copy(
-        out=dst.rearrange("p (c i) j -> p c j i", i=4),
-        in_=src.rearrange("p j (c i) -> p c j i", i=4),
-    )
-
-
-def quantize(nc, codes, scales, src):
-    nc.vector.quantize_mx(out=codes.bitcast(FP8X4), scales=scales, in_=src.rearrange("p n j -> p (n j)"))
+def views(dst, src):
+    return dst.rearrange("p (c i) j -> p c j i", i=4), src.rearrange("p j (c i) -> p c j i", i=4)
 
 
 def tile_rows_glin_sigmoid_res_kernel(tc, x, w, r, out):
@@ -52,10 +36,10 @@ def tile_rows_glin_sigmoid_res_kernel(tc, x, w, r, out):
         ps = ctx.enter_context(tc.psum_pool(name="ps", bufs=1))
         ctx.enter_context(tc.manual_schedule())
 
-        x_raw = [sb.tile([P, PACK, HALF], F32, name="x_raw%d" % h) for h in range(HALVES)]
+        x_first = sb.tile([P, PACK, FIRST], F32)
+        x_rest = sb.tile([P, PACK, N - FIRST], F32)
         w_raw = sb.tile([P, PACK, M], F32)
         r_sb = [sb.tile([P, 2, HALF], F32, name="r_sb%d" % i) for i in range(len(PIECES))]
-        x_bf = [sb.tile([P, HALF, PACK], BF16, name="x_bf%d" % h, align_bytes=64) for h in range(HALVES)]
         w_bf = sb.tile([P, M, PACK], BF16, align_bytes=64)
         x_codes = [sb.tile([P, HALF], U32, name="x_codes%d" % h, align_bytes=64) for h in range(HALVES)]
         x_scales = [sb.tile([P, HALF], U8, name="x_scales%d" % h, align_bytes=64) for h in range(HALVES)]
@@ -64,9 +48,29 @@ def tile_rows_glin_sigmoid_res_kernel(tc, x, w, r, out):
         sig = [sb.tile([P, 2, HALF], F32, name="sig%d" % i) for i in range(len(PIECES))]
         res = [sb.tile([P, 2, HALF], F32, name="res%d" % i) for i in range(len(PIECES))]
         z = [[ps.tile([P, HALF], F32, name="z%d_%d" % (g, h)) for h in range(HALVES)] for g in range(G)]
+        x_bf = {}
 
         def cols(h):
             return slice(h * HALF, (h + 1) * HALF)
+
+        def piece_of(t, i):
+            (g0, h0), (g1, h1) = PIECES[i]
+            if g0 == g1:
+                return t[g0].rearrange("m (h n) -> m h n", h=HALVES)
+            return t[g0 : g1 + 1, :, cols(h0)].rearrange("g m n -> m g n")
+
+        def interleave_x(copy, n0, n1):
+            raw = x_first[:, :, n0:n1] if n0 < FIRST else x_rest[:, :, n0 - FIRST : n1 - FIRST]
+            x_bf[n0] = sb.tile([P, n1 - n0, PACK], BF16, name="x_bf%d" % n0, align_bytes=64)
+            copy(*views(x_bf[n0][:], raw))
+
+        def quantize(codes, scales, src):
+            nc.vector.quantize_mx(out=codes.bitcast(FP8X4), scales=scales, in_=src.rearrange("p n j -> p (n j)"))
+
+        def quantize_x(n0, n1):
+            h = n0 // HALF
+            part = slice(n0 - h * HALF, n1 - h * HALF)
+            quantize(x_codes[h][:, part], x_scales[h][:, part], x_bf[n0][:])
 
         def matmul(g, h):
             rows = slice(g * ROWS, (g + 1) * ROWS)
@@ -80,43 +84,34 @@ def tile_rows_glin_sigmoid_res_kernel(tc, x, w, r, out):
                 stop=True,
             )
 
-        def piece_of(t, i):
-            (g0, h0), (g1, h1) = PIECES[i]
-            if g0 == g1:
-                return t[g0].rearrange("m (h n) -> m h n", h=HALVES)
-            return t[g0 : g1 + 1, :, cols(h0)].rearrange("g m n -> m g n")
-
-        nc.sync.dma_start(out=x_raw[0][:], in_=x_rows[:, :, cols(0)])
+        nc.sync.dma_start(out=x_first[:], in_=x_rows[:, :, :FIRST])
         nc.sync.dma_start(out=w_raw[:], in_=w_rows)
-        nc.sync.dma_start(out=x_raw[1][:], in_=x_rows[:, :, cols(1)])
+        nc.sync.dma_start(out=x_rest[:], in_=x_rows[:, :, FIRST:])
         for i in range(len(PIECES)):
             nc.sync.dma_start(out=r_sb[i][:], in_=piece_of(r, i))
-
-        def prepare(h):
-            for part in (slice(0, QUART), slice(QUART, HALF)):
-                interleave(nc, x_bf[h][:, part, :], x_raw[h][:, :, part])
-
-        def finish(h, part):
-            quantize(nc, x_codes[h][:, part], x_scales[h][:, part], x_bf[h][:, part, :])
 
         warm = sb.tile([P, 8], F32)
         nc.gpsimd.memset(warm[:], 0.0)
         nc.scalar.activation(out=warm[:], in_=warm[:], func=SIGMOID)
-        prepare(0)
-        interleave(nc, w_bf[:], w_raw[:])
-        finish(0, slice(0, HALF))
-        quantize(nc, w_codes[:], w_scales[:], w_bf[:])
-        interleave_s(nc, x_bf[1][:, SPLIT:, :], x_raw[1][:, :, SPLIT:])
-        for g in range(G):
-            matmul(g, 0)
-        for part in (slice(0, QUART), slice(QUART, SPLIT)):
-            interleave(nc, x_bf[1][:, part, :], x_raw[1][:, :, part])
-        finish(1, slice(0, QUART))
-        finish(1, slice(QUART, HALF))
+
+        on_v, on_s = nc.vector.tensor_copy, nc.scalar.copy
+        interleave_x(on_v, 0, 256)
+        interleave_x(on_s, 256, 512)
+        interleave_x(on_s, 512, 640)
+        on_v(*views(w_bf[:], w_raw[:]))
+        quantize_x(0, 256)
+        quantize(w_codes[:], w_scales[:], w_bf[:])
+        quantize_x(256, 512)
+        quantize_x(512, 640)
+        interleave_x(on_v, 640, 896)
+        interleave_x(on_v, 896, 960)
+        interleave_x(on_s, 960, 1024)
+        quantize_x(640, 896)
+        quantize_x(960, 1024)
+        quantize_x(896, 960)
         for i, piece in enumerate(PIECES):
             for s, (g, h) in enumerate(piece):
-                if h == 1:
-                    matmul(g, h)
+                matmul(g, h)
                 nc.scalar.activation(out=sig[i][:, s, :], in_=z[g][h][:], func=SIGMOID)
                 nc.vector.tensor_tensor(out=res[i][:, s, :], in0=sig[i][:, s, :], in1=r_sb[i][:, s, :], op=ADD)
-            nc.sync.dma_start(out=piece_of(out, i), in_=res[i][:])
+                nc.sync.dma_start(out=out[g][:, cols(h)], in_=res[i][:, s, :])

from contextlib import ExitStack

import concourse.mybir as mybir

G, D, M, N = 4, 128, 128, 1024
FLOPS = 2 * G * D * M * N

F32 = mybir.dt.float32
BF16 = mybir.dt.bfloat16
U32 = mybir.dt.uint32
U8 = mybir.dt.uint8
FP8X4 = mybir.dt.float8_e4m3fn_x4
SIGMOID = mybir.ActivationFunctionType.Sigmoid
ADD = mybir.AluOpType.add

P = 128
PACK = 4
ROWS = D // PACK
HALF = 512
HALVES = N // HALF
FIRST = 640
PIECES = (((0, 0), (1, 0)), ((2, 0), (2, 1)), ((3, 0), (3, 1)), ((0, 1), (1, 1)))


def views(dst, src):
    return dst.rearrange("p (c i) j -> p c j i", i=4), src.rearrange("p j (c i) -> p c j i", i=4)


def tile_rows_glin_sigmoid_res_kernel(tc, x, w, r, out):
    nc = tc.nc
    x_rows = x.rearrange("g (p j) n -> (g p) j n", j=PACK)
    w_rows = w.rearrange("g (p j) m -> (g p) j m", j=PACK)

    with ExitStack() as ctx:
        sb = ctx.enter_context(tc.tile_pool(name="sb", bufs=1))
        ps = ctx.enter_context(tc.psum_pool(name="ps", bufs=1))
        ctx.enter_context(tc.manual_schedule())

        x_first = sb.tile([P, PACK, FIRST], F32)
        x_rest = sb.tile([P, PACK, N - FIRST], F32)
        w_raw = sb.tile([P, PACK, M], F32)
        r_sb = [sb.tile([P, 2, HALF], F32, name="r_sb%d" % i) for i in range(len(PIECES))]
        w_bf = sb.tile([P, M, PACK], BF16, align_bytes=64)
        x_codes = [sb.tile([P, HALF], U32, name="x_codes%d" % h, align_bytes=64) for h in range(HALVES)]
        x_scales = [sb.tile([P, HALF], U8, name="x_scales%d" % h, align_bytes=64) for h in range(HALVES)]
        w_codes = sb.tile([P, M], U32, align_bytes=64)
        w_scales = sb.tile([P, M], U8, align_bytes=64)
        sig = [sb.tile([P, 2, HALF], F32, name="sig%d" % i) for i in range(len(PIECES))]
        res = [sb.tile([P, 2, HALF], F32, name="res%d" % i) for i in range(len(PIECES))]
        z = [[ps.tile([P, HALF], F32, name="z%d_%d" % (g, h)) for h in range(HALVES)] for g in range(G)]
        x_bf = {}

        def cols(h):
            return slice(h * HALF, (h + 1) * HALF)

        def piece_of(t, i):
            (g0, h0), (g1, h1) = PIECES[i]
            if g0 == g1:
                return t[g0].rearrange("m (h n) -> m h n", h=HALVES)
            return t[g0 : g1 + 1, :, cols(h0)].rearrange("g m n -> m g n")

        def interleave_x(copy, n0, n1):
            raw = x_first[:, :, n0:n1] if n0 < FIRST else x_rest[:, :, n0 - FIRST : n1 - FIRST]
            x_bf[n0] = sb.tile([P, n1 - n0, PACK], BF16, name="x_bf%d" % n0, align_bytes=64)
            copy(*views(x_bf[n0][:], raw))

        def quantize(codes, scales, src):
            nc.vector.quantize_mx(out=codes.bitcast(FP8X4), scales=scales, in_=src.rearrange("p n j -> p (n j)"))

        def quantize_x(n0, n1):
            h = n0 // HALF
            part = slice(n0 - h * HALF, n1 - h * HALF)
            quantize(x_codes[h][:, part], x_scales[h][:, part], x_bf[n0][:])

        def matmul(g, h):
            rows = slice(g * ROWS, (g + 1) * ROWS)
            nc.tensor.matmul_mx(
                out=z[g][h][:],
                lhsT=w_codes[rows, :].bitcast(FP8X4),
                lhsT_scale=w_scales[rows, :],
                rhs=x_codes[h][rows, :].bitcast(FP8X4),
                rhs_scale=x_scales[h][rows, :],
                start=True,
                stop=True,
            )

        nc.sync.dma_start(out=x_first[:], in_=x_rows[:, :, :FIRST])
        nc.sync.dma_start(out=w_raw[:], in_=w_rows)
        nc.sync.dma_start(out=x_rest[:], in_=x_rows[:, :, FIRST:])
        for i in range(len(PIECES)):
            nc.sync.dma_start(out=r_sb[i][:], in_=piece_of(r, i))

        warm = sb.tile([P, 8], F32)
        nc.gpsimd.memset(warm[:], 0.0)
        nc.scalar.activation(out=warm[:], in_=warm[:], func=SIGMOID)

        on_v, on_s = nc.vector.tensor_copy, nc.scalar.copy
        interleave_x(on_v, 0, 256)
        interleave_x(on_s, 256, 512)
        interleave_x(on_s, 512, 640)
        on_v(*views(w_bf[:], w_raw[:]))
        quantize_x(0, 256)
        quantize(w_codes[:], w_scales[:], w_bf[:])
        quantize_x(256, 512)
        quantize_x(512, 640)
        interleave_x(on_v, 640, 896)
        interleave_x(on_v, 896, 960)
        interleave_x(on_s, 960, 1024)
        quantize_x(640, 896)
        quantize_x(960, 1024)
        quantize_x(896, 960)
        for i, piece in enumerate(PIECES):
            for s, (g, h) in enumerate(piece):
                matmul(g, h)
                nc.scalar.activation(out=sig[i][:, s, :], in_=z[g][h][:], func=SIGMOID)
                nc.vector.tensor_tensor(out=res[i][:, s, :], in0=sig[i][:, s, :], in1=r_sb[i][:, s, :], op=ADD)
                nc.sync.dma_start(out=out[g][:, cols(h)], in_=res[i][:, s, :])
